import numpy as np
import ml_dtypes


def mxq(x, axis, fmt="e4m3"):
    dtype, down = {"e4m3": (ml_dtypes.float8_e4m3fn, 7), "e5m2": (ml_dtypes.float8_e5m2, 14)}[fmt]
    v = np.moveaxis(np.asarray(x, np.float32).astype(ml_dtypes.bfloat16).astype(np.float64), axis, -1)
    blocks = v.reshape(v.shape[:-1] + (-1, 32))
    amax = np.abs(blocks).max(-1, keepdims=True)
    byte = np.maximum(np.where(amax > 0, np.frexp(amax)[1] - 1 + 127, 0) - down, 1)
    scale = np.exp2(byte - 127.0)
    codes = (blocks / scale).astype(np.float32).astype(dtype).astype(np.float64)
    return np.moveaxis((codes * scale).reshape(v.shape), -1, axis)


WIDE = False


def mx_kscale(k):
    if not WIDE:
        return np.ones(k)
    levels = np.array([30, -30])
    if k % 512:
        return np.exp2(np.random.permutation(np.resize(levels, k // 32))).repeat(32)
    a = np.empty((k // 512, 16))
    for p in range(k // 512):
        a[p, :8] = np.random.permutation(np.resize(levels, 8))
        for g in range(8):
            far = levels[np.abs(levels - a[p, g]) >= 10]
            a[p, g + 8] = far[np.random.randint(len(far))]
    return np.exp2(a.ravel()).repeat(32)


def f64(x):
    return np.asarray(x).astype(np.float64)


def striped(idx):
    return np.tile(np.asarray(idx).reshape(-1, 16).T, (8, 1)).astype(np.uint16)


def unstriped(offs):
    return offs[:16].T.reshape(-1).astype(np.int64)


def striped8(idx):
    return np.asarray(idx).reshape(8, -1, 16).transpose(0, 2, 1).reshape(128, -1).astype(np.uint16)


def unstriped8(offs):
    return offs.reshape(8, 16, -1).transpose(0, 2, 1).reshape(8, -1).astype(np.int64)


def pick8(x, idx, run):
    r = np.arange(len(x))
    return x[r[:, None], idx[r % (8 * run) // run]]


E2M1 = np.array([0.0, 0.5, 1.0, 1.5, 2.0, 3.0, 4.0, 6.0, -0.0, -0.5, -1.0, -1.5, -2.0, -3.0, -4.0, -6.0])


def pack_weight(w, fmt):
    k, n = w.shape
    w = f64(np.asarray(w, np.float32).astype(ml_dtypes.bfloat16)).reshape(k // 32, 32, n)
    amax = np.abs(w).max(1)
    if fmt in ("e4m3", "e5m2"):
        byte = np.frexp(amax)[1] - 1 + 127 - (7 if fmt == "e4m3" else 14)
    else:
        mant, ex = np.frexp(amax / 6.0)
        byte = np.where(mant > 0.5, ex, ex - 1) + 127
    byte = np.clip(np.where(amax > 0, byte, 1), 1, 254)
    scaled = (w * np.exp2(127.0 - byte)[:, None, :]).reshape(k, n).astype(np.float32)
    by_word = np.ascontiguousarray(scaled.reshape(k // 512, 128, 4, n).transpose(0, 1, 3, 2))
    if fmt in ("e4m3", "e5m2"):
        words = by_word.astype(ml_dtypes.float8_e4m3fn if fmt == "e4m3" else ml_dtypes.float8_e5m2).view(np.uint8)
    else:
        c = by_word.astype(ml_dtypes.float4_e2m1fn).view(np.uint8) & 0xF
        words = (c[..., 0::2] | (c[..., 1::2] << 4)).reshape(k // 512, 128, 2 * n)
    return np.ascontiguousarray(words), np.ascontiguousarray(byte.astype(np.uint8).reshape(k // 512, 16, n))


def unpack_weight(words, scales, fmt):
    g, _, n = scales.shape
    words = np.ascontiguousarray(words).reshape(g, 128, n, -1)
    if fmt in ("e4m3", "e5m2"):
        vals = words.view(ml_dtypes.float8_e4m3fn if fmt == "e4m3" else ml_dtypes.float8_e5m2).astype(np.float64)
    else:
        nib = np.empty((g, 128, n, 4), np.uint8)
        nib[..., 0::2] = words & 0xF
        nib[..., 1::2] = words >> 4
        vals = E2M1[nib]
    vals = vals * np.repeat(np.exp2(scales.astype(np.float64) - 127.0), 8, axis=1)[..., None]
    return vals.transpose(0, 1, 3, 2).reshape(g * 512, n)


def sigmoid(v):
    return 1.0 / (1.0 + np.exp(-v))


def sgn(shape):
    return np.random.uniform(0.5, 2.0, shape) * np.where(np.random.standard_normal(shape) < 0, -1.0, 1.0)


K, T, J, R, C, O, N = 512, 2048, 256, 512, 512, 128, 256


def setup_inputs():
    n = np.random.standard_normal
    idx = np.random.permutation(T)[:J]
    idx2 = np.random.permutation(T)[:J]
    idx3 = np.stack([np.random.permutation(C)[:J] for _ in range(8)])
    idx4 = np.random.permutation(C)[:O]
    idx5 = np.stack([np.random.permutation(J)[:O] for _ in range(8)])
    fk = mx_kscale(K)
    fr = mx_kscale(R)
    xtp = pack_weight(n((K, T)) / fk[:, None], "e4m3")
    wp = pack_weight(n((K, R)) * 1 / np.sqrt(K) * fk[:, None] * fr, "e2m1")
    w2p = pack_weight(n((K, R)) * 1 / np.sqrt(K) * fk[:, None], "e5m2")
    wbp = pack_weight(n((R, N)) * 1 / np.sqrt(R) / fr[:, None], "e5m2")
    return {
        "xt_words": xtp[0],
        "xt_scales": xtp[1],
        "w_words": wp[0],
        "w_scales": wp[1],
        "w2_words": w2p[0],
        "w2_scales": w2p[1],
        "sa": (sgn((R, 1))).astype(np.float32),
        "sg": (sgn((R, 1))).astype(np.float32),
        "bg": (np.random.uniform(-2.0, 2.0, (R, 1))).astype(np.float32),
        "wb_words": wbp[0],
        "wb_scales": wbp[1],
        "offs": striped(idx),
        "offs2": striped(idx2),
        "offs3": striped8(idx3),
        "offs4": striped(idx4),
        "offs5": striped8(idx5),
    }


def reference(xt_words, xt_scales, w_words, w_scales, w2_words, w2_scales, sa, sg, bg, wb_words, wb_scales, offs, offs2, offs3, offs4, offs5):
    idx = unstriped(offs)
    idx2 = unstriped(offs2)
    idx3 = unstriped8(offs3)
    idx4 = unstriped(offs4)
    idx5 = unstriped8(offs5)
    xtu = unpack_weight(xt_words, xt_scales, "e4m3")
    wu = unpack_weight(w_words, w_scales, "e2m1")
    w2u = unpack_weight(w2_words, w2_scales, "e5m2")
    wbu = unpack_weight(wb_words, wb_scales, "e5m2")
    xtidxg = xtu[:, idx]
    a = wu.T @ xtidxg
    xtidx2g = xtu[:, idx2]
    b = w2u.T @ xtidx2g
    pa = np.zeros((R, C))
    pa[np.arange(R)[:, None], idx3[np.arange(R) % 512 // 64]] = a
    hid = pa[:, idx4] * f64(sa) * sigmoid(pick8(b, idx5, 64) * f64(sg) + f64(bg))
    hidq = mxq(hid, 0, "e4m3")
    p = wbu.T @ hidq
    return p

@@ -1,0 +1,207 @@
+from contextlib import ExitStack
+
+import concourse.mybir as mybir
+
+K, T, J, R, C, O, N = 512, 2048, 256, 512, 512, 128, 256
+FLOPS = 2 * K * R * J * 2 + 2 * R * N * O
+
+P = 128
+PACK = 4
+QUADS = 4
+QUAD = 32
+LINE = 16
+
+F32 = mybir.dt.float32
+BF16 = mybir.dt.bfloat16
+I32 = mybir.dt.int32
+U32 = mybir.dt.uint32
+U16 = mybir.dt.uint16
+U8 = mybir.dt.uint8
+E4M3 = mybir.dt.float8_e4m3fn_x4
+E5M2 = mybir.dt.float8_e5m2_x4
+E2M1 = mybir.dt.float4_e2m1fn_x4
+ACT = mybir.ActivationFunctionType
+ALU = mybir.AluOpType
+
+
+def load_scale_rows(nc, plane, scales):
+    for q in range(QUADS):
+        nc.sync.dma_start(
+            out=plane[QUAD * q : QUAD * q + PACK, :].bitcast(I32),
+            in_=scales[0, PACK * q : PACK * (q + 1), :].bitcast(I32),
+        )
+
+
+def deal_views(dst, src, run):
+    return (
+        dst.rearrange("p (t c i) -> p c t i", t=PACK, i=run),
+        src.rearrange("p (c i t) -> p c t i", t=PACK, i=run),
+    )
+
+
+def tile_list_gatedbyslots_kernel(
+    tc, xt_words, xt_scales, w_words, w_scales, w2_words, w2_scales, sa, sg, bg,
+    wb_words, wb_scales, offs, offs2, offs3, offs4, offs5, out,
+):
+    nc = tc.nc
+    with ExitStack() as ctx:
+        sb = ctx.enter_context(tc.tile_pool(name="sb", bufs=1))
+        ps = ctx.enter_context(tc.psum_pool(name="ps", bufs=1))
+
+        x_words = sb.tile([P, T], I32, name="x_words", align_bytes=64)
+        x_plane = sb.tile([P, T], U8, name="x_plane", align_bytes=64)
+        w_raw = sb.tile([P, 2 * R], U8, name="w_raw", align_bytes=64)
+        w_rows = sb.tile([PACK, QUADS, R // 4], I32, name="w_rows", align_bytes=64)
+        w_plane_raw = sb.tile([P, R], U8, name="w_plane_raw", align_bytes=64)
+        w2_raw = sb.tile([P, R], I32, name="w2_raw", align_bytes=64)
+        w2_plane_raw = sb.tile([P, R], U8, name="w2_plane_raw", align_bytes=64)
+        wb_codes = sb.tile([P, N], I32, name="wb_codes", align_bytes=64)
+        wb_plane = sb.tile([P, N], U8, name="wb_plane", align_bytes=64)
+        list1 = sb.tile([P, J // 16], U16, name="list1")
+        list2 = sb.tile([P, J // 16], U16, name="list2")
+        list3 = sb.tile([P, J // 16], U16, name="list3")
+        list4 = sb.tile([P, O // 16], U16, name="list4")
+        list5 = sb.tile([P, O // 16], U16, name="list5")
+        sa_t = sb.tile([P, PACK], F32, name="sa_t")
+        sg_t = sb.tile([P, PACK], F32, name="sg_t")
+        bg_t = sb.tile([P, PACK], F32, name="bg_t")
+        boards = [sb.tile([P, C], F32, name="board%d" % t, align_bytes=64) for t in range(PACK)]
+
+        nc.vector.memset(x_plane[:].bitcast(I32), 0)
+        nc.vector.memset(w_plane_raw[:].bitcast(I32), 0)
+        nc.vector.memset(w2_plane_raw[:].bitcast(I32), 0)
+        nc.vector.memset(wb_plane[:].bitcast(I32), 0)
+        for t in range(PACK):
+            nc.vector.memset(boards[t][:], 0.0)
+
+        nc.scalar.dma_start(out=x_words[:], in_=xt_words[0].rearrange("p n t -> p (n t)").bitcast(I32))
+        nc.sync.dma_start(list1[:], offs)
+        nc.sync.dma_start(out=w_rows[:], in_=w_scales[0].bitcast(I32).rearrange("(q r) n -> r q n", r=PACK))
+        nc.sync.dma_start(out=w_raw[:].bitcast(I32), in_=w_words[0].bitcast(I32))
+        load_scale_rows(nc, x_plane, xt_scales)
+        nc.sync.dma_start(list3[:], offs3)
+        nc.sync.dma_start(list2[:], offs2)
+        load_scale_rows(nc, w2_plane_raw, w2_scales)
+        nc.sync.dma_start(out=w2_raw[:], in_=w2_words[0].rearrange("p n t -> p (n t)").bitcast(I32))
+        nc.sync.dma_start(list4[:], offs4)
+        nc.sync.dma_start(out=sa_t[:], in_=sa.rearrange("(p t) o -> p (t o)", t=PACK))
+        nc.sync.dma_start(list5[:], offs5)
+        nc.sync.dma_start(out=sg_t[:], in_=sg.rearrange("(p t) o -> p (t o)", t=PACK))
+        nc.sync.dma_start(out=bg_t[:], in_=bg.rearrange("(p t) o -> p (t o)", t=PACK))
+        load_scale_rows(nc, wb_plane, wb_scales)
+        nc.sync.dma_start(out=wb_codes[:], in_=wb_words[0].rearrange("p n t -> p (n t)").bitcast(I32))
+
+        w_codes = sb.tile([P, R], U16, name="w_codes", align_bytes=64)
+        w_plane = sb.tile([P, R], U8, name="w_plane", align_bytes=64)
+        for q in range(QUADS):
+            nc.vector.tensor_copy(out=w_plane_raw[QUAD * q : QUAD * q + PACK, :].bitcast(I32), in_=w_rows[:, q, :])
+        dst, src = deal_views(w_plane[:], w_plane_raw[:], LINE)
+        nc.vector.tensor_copy(out=dst, in_=src)
+        dst, src = deal_views(w_codes[:], w_raw[:].bitcast(U16), LINE // 2)
+        nc.scalar.copy(out=dst, in_=src)
+
+        x1_plane = sb.tile([P, J], U8, name="x1_plane", align_bytes=64)
+        x1_words = sb.tile([P, J], U32, name="x1_words", align_bytes=64)
+        nc.vector.tensor_copy(out=x1_plane[:], in_=x_plane[:].indirect(list1[:]))
+        nc.vector.tensor_copy(out=x1_words[:], in_=x_words[:].bitcast(U32).indirect(list1[:]))
+
+        def first_product(bank, t, cols):
+            nc.tensor.matmul_mx(
+                out=bank,
+                lhsT=w_codes[:, P * t : P * (t + 1)].bitcast(E2M1),
+                lhsT_scale=w_plane[:, P * t : P * (t + 1)],
+                rhs=x1_words[:, cols].bitcast(E4M3),
+                rhs_scale=x1_plane[:, cols],
+                start=True,
+                stop=True,
+            )
+
+        a_rows = [sb.tile([P, J], F32, name="a%d" % t, align_bytes=64) for t in range(PACK)]
+        half = J // 2
+        a0_lo = ps.tile([P, half], F32, name="a0_lo")
+        a0_hi = ps.tile([P, half], F32, name="a0_hi")
+        a1_bank = ps.tile([P, J], F32, name="a1_bank")
+        a23_bank = ps.tile([P, 2, J], F32, name="a23_bank")
+        first_product(a0_lo[:], 0, slice(0, half))
+        first_product(a0_hi[:], 0, slice(half, J))
+        nc.scalar.copy(out=a_rows[0][:, 0:half], in_=a0_lo[:])
+        nc.vector.tensor_copy(out=a_rows[0][:, half:J], in_=a0_hi[:])
+        first_product(a1_bank[:], 1, slice(0, J))
+        nc.vector.tensor_copy(out=a_rows[1][:], in_=a1_bank[:])
+        for t in (2, 3):
+            first_product(a23_bank[:, t - 2, :], t, slice(0, J))
+        for t in (2, 3):
+            nc.vector.tensor_copy(out=a_rows[t][:], in_=a23_bank[:, t - 2, :])
+        for t in range(PACK):
+            nc.scalar.activation(out=boards[t][:].indirect(list3[:]), in_=a_rows[t][:], func=ACT.Copy)
+
+        w2_codes = sb.tile([P, R], I32, name="w2_codes", align_bytes=64)
+        w2_plane = sb.tile([P, R], U8, name="w2_plane", align_bytes=64)
+        x2_plane = sb.tile([P, J], U8, name="x2_plane", align_bytes=64)
+        x2_words = sb.tile([P, J], U32, name="x2_words", align_bytes=64)
+        nc.vector.tensor_copy(out=x2_plane[:], in_=x_plane[:].indirect(list2[:]))
+        nc.vector.tensor_copy(out=x2_words[:], in_=x_words[:].bitcast(U32).indirect(list2[:]))
+        dst, src = deal_views(w2_plane[:], w2_plane_raw[:], LINE)
+        nc.vector.tensor_copy(out=dst, in_=src)
+        dst, src = deal_views(w2_codes[:], w2_raw[:], LINE // 4)
+        nc.vector.tensor_copy(out=dst, in_=src)
+        b_rows = [sb.tile([P, J], F32, name="b%d" % t, align_bytes=64) for t in range(PACK)]
+        for pair in range(2):
+            b_bank = ps.tile([P, 2, J], F32, name="b_bank%d" % pair)
+            for u in range(2):
+                t = 2 * pair + u
+                nc.tensor.matmul_mx(
+                    out=b_bank[:, u, :],
+                    lhsT=w2_codes[:, P * t : P * (t + 1)].bitcast(E5M2),
+                    lhsT_scale=w2_plane[:, P * t : P * (t + 1)],
+                    rhs=x2_words[:].bitcast(E4M3),
+                    rhs_scale=x2_plane[:],
+                    start=True,
+                    stop=True,
+                )
+            for u in range(2):
+                nc.vector.tensor_copy(out=b_rows[2 * pair + u][:], in_=b_bank[:, u, :])
+
+        hid = sb.tile([P, O, PACK], BF16, name="hid", align_bytes=64)
+        for pair in range(2):
+            picked = sb.tile([P, 2, O], F32, name="picked%d" % pair, align_bytes=64)
+            gate = sb.tile([P, 2, O], F32, name="gate%d" % pair, align_bytes=64)
+            for u in range(2):
+                t = 2 * pair + u
+                nc.scalar.activation(
+                    out=picked[:, u, :], in_=boards[t][:].indirect(list4[:]), func=ACT.Copy, scale=sa_t[:, t : t + 1],
+                )
+                nc.scalar.activation(
+                    out=gate[:, u, :], in_=b_rows[t][:].indirect(list5[:]), func=ACT.Sigmoid,
+                    bias=bg_t[:, t : t + 1], scale=sg_t[:, t : t + 1],
+                )
+            nc.vector.tensor_tensor(
+                out=hid[:, :, 2 * pair : 2 * pair + 2],
+                in0=picked[:].rearrange("p u o -> p o u"),
+                in1=gate[:].rearrange("p u o -> p o u"),
+                op=ALU.mult,
+            )
+
+        hid_codes = sb.tile([P, O], U32, name="hid_codes", align_bytes=64)
+        hid_plane = sb.tile([P, O], U8, name="hid_plane", align_bytes=64)
+        nc.vector.quantize_mx(
+            out=hid_codes[:].bitcast(E4M3), scales=hid_plane[:], in_=hid[:].rearrange("p o t -> p (o t)")
+        )
+        for h in range(N // P):
+            o_bank = ps.tile([P, O], F32, name="o_bank%d" % h)
+            result = sb.tile([P, O], F32, name="result%d" % h, align_bytes=64)
+            nc.tensor.matmul_mx(
+                out=o_bank[:],
+                lhsT=wb_codes[:, P * h : P * (h + 1)].bitcast(E5M2),
+                lhsT_scale=wb_plane[:, P * h : P * (h + 1)],
+                rhs=hid_codes[:].bitcast(E4M3),
+                rhs_scale=hid_plane[:],
+                start=True,
+                stop=True,
+            )
+            if h == 0:
+                nc.scalar.copy(out=result[:], in_=o_bank[:])
+                nc.scalar.dma_start(out=out[P * h : P * (h + 1), :], in_=result[:])
+            else:
+                nc.vector.tensor_copy(out=result[:], in_=o_bank[:])
+                nc.sync.dma_start(out=out[P * h : P * (h + 1), :], in_=result[:])

@@ -75,6 +75,10 @@ def tile_list_gatedbyslots_kernel(
             nc.vector.memset(boards[t][:], 0.0)
 
         nc.scalar.dma_start(out=x_words[:], in_=xt_words[0].rearrange("p n t -> p (n t)").bitcast(I32))
+        warm_in = sb.tile([P, 1], F32, name="warm_in")
+        warm_out = sb.tile([P, 1], F32, name="warm_out")
+        nc.gpsimd.memset(warm_in[:], 0.0)
+        nc.scalar.activation(out=warm_out[:], in_=warm_in[:], func=ACT.Sigmoid)
         nc.sync.dma_start(list1[:], offs)
         nc.sync.dma_start(out=w_rows[:], in_=w_scales[0].bitcast(I32).rearrange("(q r) n -> r q n", r=PACK))
         nc.sync.dma_start(out=w_raw[:].bitcast(I32), in_=w_words[0].bitcast(I32))

@@ -74,12 +74,12 @@ def tile_list_gatedbyslots_kernel(
         for t in range(PACK):
             nc.vector.memset(boards[t][:], 0.0)
 
+        nc.sync.dma_start(list1[:], offs)
         nc.scalar.dma_start(out=x_words[:], in_=xt_words[0].rearrange("p n t -> p (n t)").bitcast(I32))
         warm_in = sb.tile([P, 1], F32, name="warm_in")
         warm_out = sb.tile([P, 1], F32, name="warm_out")
         nc.gpsimd.memset(warm_in[:], 0.0)
         nc.scalar.activation(out=warm_out[:], in_=warm_in[:], func=ACT.Sigmoid)
-        nc.sync.dma_start(list1[:], offs)
         nc.sync.dma_start(out=w_rows[:], in_=w_scales[0].bitcast(I32).rearrange("(q r) n -> r q n", r=PACK))
         nc.sync.dma_start(out=w_raw[:].bitcast(I32), in_=w_words[0].bitcast(I32))
         load_scale_rows(nc, x_plane, xt_scales)
@@ -167,30 +167,47 @@ def tile_list_gatedbyslots_kernel(
                 nc.vector.tensor_copy(out=b_rows[2 * pair + u][:], in_=b_bank[:, u, :])
 
         hid = sb.tile([P, O, PACK], BF16, name="hid", align_bytes=64)
-        for pair in range(2):
-            picked = sb.tile([P, 2, O], F32, name="picked%d" % pair, align_bytes=64)
-            gate = sb.tile([P, 2, O], F32, name="gate%d" % pair, align_bytes=64)
-            for u in range(2):
-                t = 2 * pair + u
-                nc.scalar.activation(
-                    out=picked[:, u, :], in_=boards[t][:].indirect(list4[:]), func=ACT.Copy, scale=sa_t[:, t : t + 1],
-                )
-                nc.scalar.activation(
-                    out=gate[:, u, :], in_=b_rows[t][:].indirect(list5[:]), func=ACT.Sigmoid,
-                    bias=bg_t[:, t : t + 1], scale=sg_t[:, t : t + 1],
-                )
+        hid_codes = sb.tile([P, O], U32, name="hid_codes", align_bytes=64)
+        hid_plane = sb.tile([P, O], U8, name="hid_plane", align_bytes=64)
+        picked = [sb.tile([P, 2, O], F32, name="picked%d" % pair, align_bytes=64) for pair in range(2)]
+        gate = [sb.tile([P, 2, O], F32, name="gate%d" % pair, align_bytes=64) for pair in range(2)]
+
+        def pick(t):
+            nc.scalar.activation(
+                out=picked[t // 2][:, t % 2, :], in_=boards[t][:].indirect(list4[:]), func=ACT.Copy,
+                scale=sa_t[:, t : t + 1],
+            )
+
+        def look(t, lo, hi):
+            nc.scalar.activation(
+                out=gate[t // 2][:, t % 2, lo:hi], in_=b_rows[t][:].indirect(list5[:, lo // 16 : hi // 16]),
+                func=ACT.Sigmoid, bias=bg_t[:, t : t + 1], scale=sg_t[:, t : t + 1],
+            )
+
+        def join(pair, lo, hi):
             nc.vector.tensor_tensor(
-                out=hid[:, :, 2 * pair : 2 * pair + 2],
-                in0=picked[:].rearrange("p u o -> p o u"),
-                in1=gate[:].rearrange("p u o -> p o u"),
+                out=hid[:, lo:hi, 2 * pair : 2 * pair + 2],
+                in0=picked[pair][:, :, lo:hi].rearrange("p u o -> p o u"),
+                in1=gate[pair][:, :, lo:hi].rearrange("p u o -> p o u"),
                 op=ALU.mult,
             )
 
-        hid_codes = sb.tile([P, O], U32, name="hid_codes", align_bytes=64)
-        hid_plane = sb.tile([P, O], U8, name="hid_plane", align_bytes=64)
-        nc.vector.quantize_mx(
-            out=hid_codes[:].bitcast(E4M3), scales=hid_plane[:], in_=hid[:].rearrange("p o t -> p (o t)")
-        )
+        halves = ((0, O // 2), (O // 2, O))
+        for t in range(PACK - 1):
+            pick(t)
+            look(t, 0, O)
+            if t == 1:
+                join(0, 0, O)
+        pick(PACK - 1)
+        for lo, hi in halves:
+            look(PACK - 1, lo, hi)
+            join(1, lo, hi)
+        for lo, hi in halves:
+            nc.vector.quantize_mx(
+                out=hid_codes[:, lo:hi].bitcast(E4M3),
+                scales=hid_plane[:, lo:hi],
+                in_=hid[:, lo:hi, :].rearrange("p o t -> p (o t)"),
+            )
         for h in range(N // P):
             o_bank = ps.tile([P, O], F32, name="o_bank%d" % h)
             result = sb.tile([P, O], F32, name="result%d" % h, align_bytes=64)

@@ -24,9 +24,9 @@ ACT = mybir.ActivationFunctionType
 ALU = mybir.AluOpType
 
 
-def load_scale_rows(nc, plane, scales):
+def load_scale_rows(queues, plane, scales):
     for q in range(QUADS):
-        nc.sync.dma_start(
+        queues[q].dma_start(
             out=plane[QUAD * q : QUAD * q + PACK, :].bitcast(I32),
             in_=scales[0, PACK * q : PACK * (q + 1), :].bitcast(I32),
         )
@@ -67,32 +67,32 @@ def tile_list_gatedbyslots_kernel(
         bg_t = sb.tile([P, PACK], F32, name="bg_t")
         boards = [sb.tile([P, C], F32, name="board%d" % t, align_bytes=64) for t in range(PACK)]
 
+        warm_in = sb.tile([P, 1], F32, name="warm_in")
+        warm_out = sb.tile([P, 1], F32, name="warm_out")
         nc.vector.memset(x_plane[:].bitcast(I32), 0)
         nc.vector.memset(w_plane_raw[:].bitcast(I32), 0)
+        nc.vector.memset(warm_in[:], 0.0)
         nc.vector.memset(w2_plane_raw[:].bitcast(I32), 0)
         nc.vector.memset(wb_plane[:].bitcast(I32), 0)
         for t in range(PACK):
             nc.vector.memset(boards[t][:], 0.0)
 
         nc.sync.dma_start(list1[:], offs)
-        nc.scalar.dma_start(out=x_words[:], in_=xt_words[0].rearrange("p n t -> p (n t)").bitcast(I32))
-        warm_in = sb.tile([P, 1], F32, name="warm_in")
-        warm_out = sb.tile([P, 1], F32, name="warm_out")
-        nc.gpsimd.memset(warm_in[:], 0.0)
-        nc.scalar.activation(out=warm_out[:], in_=warm_in[:], func=ACT.Sigmoid)
         nc.sync.dma_start(out=w_rows[:], in_=w_scales[0].bitcast(I32).rearrange("(q r) n -> r q n", r=PACK))
         nc.sync.dma_start(out=w_raw[:].bitcast(I32), in_=w_words[0].bitcast(I32))
-        load_scale_rows(nc, x_plane, xt_scales)
+        load_scale_rows([nc.scalar, nc.sync, nc.scalar, nc.sync], x_plane, xt_scales)
+        nc.sync.dma_start(out=x_words[:], in_=xt_words[0].rearrange("p n t -> p (n t)").bitcast(I32))
+        nc.scalar.activation(out=warm_out[:], in_=warm_in[:], func=ACT.Sigmoid)
         nc.sync.dma_start(list3[:], offs3)
         nc.sync.dma_start(list2[:], offs2)
-        load_scale_rows(nc, w2_plane_raw, w2_scales)
+        load_scale_rows([nc.sync] * QUADS, w2_plane_raw, w2_scales)
         nc.sync.dma_start(out=w2_raw[:], in_=w2_words[0].rearrange("p n t -> p (n t)").bitcast(I32))
         nc.sync.dma_start(list4[:], offs4)
         nc.sync.dma_start(out=sa_t[:], in_=sa.rearrange("(p t) o -> p (t o)", t=PACK))
         nc.sync.dma_start(list5[:], offs5)
         nc.sync.dma_start(out=sg_t[:], in_=sg.rearrange("(p t) o -> p (t o)", t=PACK))
         nc.sync.dma_start(out=bg_t[:], in_=bg.rearrange("(p t) o -> p (t o)", t=PACK))
-        load_scale_rows(nc, wb_plane, wb_scales)
+        load_scale_rows([nc.sync] * QUADS, wb_plane, wb_scales)
         nc.sync.dma_start(out=wb_codes[:], in_=wb_words[0].rearrange("p n t -> p (n t)").bitcast(I32))
 
         w_codes = sb.tile([P, R], U16, name="w_codes", align_bytes=64)

from contextlib import ExitStack

import concourse.mybir as mybir

K, T, J, R, C, O, N = 512, 2048, 256, 512, 512, 128, 256
FLOPS = 2 * K * R * J * 2 + 2 * R * N * O

P = 128
PACK = 4
QUADS = 4
QUAD = 32
LINE = 16

F32 = mybir.dt.float32
BF16 = mybir.dt.bfloat16
I32 = mybir.dt.int32
U32 = mybir.dt.uint32
U16 = mybir.dt.uint16
U8 = mybir.dt.uint8
E4M3 = mybir.dt.float8_e4m3fn_x4
E5M2 = mybir.dt.float8_e5m2_x4
E2M1 = mybir.dt.float4_e2m1fn_x4
ACT = mybir.ActivationFunctionType
ALU = mybir.AluOpType


def load_scale_rows(queues, plane, scales):
    for q in range(QUADS):
        queues[q].dma_start(
            out=plane[QUAD * q : QUAD * q + PACK, :].bitcast(I32),
            in_=scales[0, PACK * q : PACK * (q + 1), :].bitcast(I32),
        )


def deal_views(dst, src, run):
    return (
        dst.rearrange("p (t c i) -> p c t i", t=PACK, i=run),
        src.rearrange("p (c i t) -> p c t i", t=PACK, i=run),
    )


def tile_list_gatedbyslots_kernel(
    tc, xt_words, xt_scales, w_words, w_scales, w2_words, w2_scales, sa, sg, bg,
    wb_words, wb_scales, offs, offs2, offs3, offs4, offs5, out,
):
    nc = tc.nc
    with ExitStack() as ctx:
        sb = ctx.enter_context(tc.tile_pool(name="sb", bufs=1))
        ps = ctx.enter_context(tc.psum_pool(name="ps", bufs=1))

        x_words = sb.tile([P, T], I32, name="x_words", align_bytes=64)
        x_plane = sb.tile([P, T], U8, name="x_plane", align_bytes=64)
        w_raw = sb.tile([P, 2 * R], U8, name="w_raw", align_bytes=64)
        w_rows = sb.tile([PACK, QUADS, R // 4], I32, name="w_rows", align_bytes=64)
        w_plane_raw = sb.tile([P, R], U8, name="w_plane_raw", align_bytes=64)
        w2_raw = sb.tile([P, R], I32, name="w2_raw", align_bytes=64)
        w2_plane_raw = sb.tile([P, R], U8, name="w2_plane_raw", align_bytes=64)
        wb_codes = sb.tile([P, N], I32, name="wb_codes", align_bytes=64)
        wb_plane = sb.tile([P, N], U8, name="wb_plane", align_bytes=64)
        list1 = sb.tile([P, J // 16], U16, name="list1")
        list2 = sb.tile([P, J // 16], U16, name="list2")
        list3 = sb.tile([P, J // 16], U16, name="list3")
        list4 = sb.tile([P, O // 16], U16, name="list4")
        list5 = sb.tile([P, O // 16], U16, name="list5")
        sa_t = sb.tile([P, PACK], F32, name="sa_t")
        sg_t = sb.tile([P, PACK], F32, name="sg_t")
        bg_t = sb.tile([P, PACK], F32, name="bg_t")
        boards = [sb.tile([P, C], F32, name="board%d" % t, align_bytes=64) for t in range(PACK)]

        warm_in = sb.tile([P, 1], F32, name="warm_in")
        warm_out = sb.tile([P, 1], F32, name="warm_out")
        nc.vector.memset(x_plane[:].bitcast(I32), 0)
        nc.vector.memset(w_plane_raw[:].bitcast(I32), 0)
        nc.vector.memset(warm_in[:], 0.0)
        nc.vector.memset(w2_plane_raw[:].bitcast(I32), 0)
        nc.vector.memset(wb_plane[:].bitcast(I32), 0)
        for t in range(PACK):
            nc.vector.memset(boards[t][:], 0.0)

        nc.sync.dma_start(list1[:], offs)
        nc.sync.dma_start(out=w_rows[:], in_=w_scales[0].bitcast(I32).rearrange("(q r) n -> r q n", r=PACK))
        nc.sync.dma_start(out=w_raw[:].bitcast(I32), in_=w_words[0].bitcast(I32))
        load_scale_rows([nc.scalar, nc.sync, nc.scalar, nc.sync], x_plane, xt_scales)
        nc.sync.dma_start(out=x_words[:], in_=xt_words[0].rearrange("p n t -> p (n t)").bitcast(I32))
        nc.scalar.activation(out=warm_out[:], in_=warm_in[:], func=ACT.Sigmoid)
        nc.sync.dma_start(list3[:], offs3)
        nc.sync.dma_start(list2[:], offs2)
        load_scale_rows([nc.sync] * QUADS, w2_plane_raw, w2_scales)
        nc.sync.dma_start(out=w2_raw[:], in_=w2_words[0].rearrange("p n t -> p (n t)").bitcast(I32))
        nc.sync.dma_start(list4[:], offs4)
        nc.sync.dma_start(out=sa_t[:], in_=sa.rearrange("(p t) o -> p (t o)", t=PACK))
        nc.sync.dma_start(list5[:], offs5)
        nc.sync.dma_start(out=sg_t[:], in_=sg.rearrange("(p t) o -> p (t o)", t=PACK))
        nc.sync.dma_start(out=bg_t[:], in_=bg.rearrange("(p t) o -> p (t o)", t=PACK))
        load_scale_rows([nc.sync] * QUADS, wb_plane, wb_scales)
        nc.sync.dma_start(out=wb_codes[:], in_=wb_words[0].rearrange("p n t -> p (n t)").bitcast(I32))

        w_codes = sb.tile([P, R], U16, name="w_codes", align_bytes=64)
        w_plane = sb.tile([P, R], U8, name="w_plane", align_bytes=64)
        for q in range(QUADS):
            nc.vector.tensor_copy(out=w_plane_raw[QUAD * q : QUAD * q + PACK, :].bitcast(I32), in_=w_rows[:, q, :])
        dst, src = deal_views(w_plane[:], w_plane_raw[:], LINE)
        nc.vector.tensor_copy(out=dst, in_=src)
        dst, src = deal_views(w_codes[:], w_raw[:].bitcast(U16), LINE // 2)
        nc.scalar.copy(out=dst, in_=src)

        x1_plane = sb.tile([P, J], U8, name="x1_plane", align_bytes=64)
        x1_words = sb.tile([P, J], U32, name="x1_words", align_bytes=64)
        nc.vector.tensor_copy(out=x1_plane[:], in_=x_plane[:].indirect(list1[:]))
        nc.vector.tensor_copy(out=x1_words[:], in_=x_words[:].bitcast(U32).indirect(list1[:]))

        def first_product(bank, t, cols):
            nc.tensor.matmul_mx(
                out=bank,
                lhsT=w_codes[:, P * t : P * (t + 1)].bitcast(E2M1),
                lhsT_scale=w_plane[:, P * t : P * (t + 1)],
                rhs=x1_words[:, cols].bitcast(E4M3),
                rhs_scale=x1_plane[:, cols],
                start=True,
                stop=True,
            )

        a_rows = [sb.tile([P, J], F32, name="a%d" % t, align_bytes=64) for t in range(PACK)]
        half = J // 2
        a0_lo = ps.tile([P, half], F32, name="a0_lo")
        a0_hi = ps.tile([P, half], F32, name="a0_hi")
        a1_bank = ps.tile([P, J], F32, name="a1_bank")
        a23_bank = ps.tile([P, 2, J], F32, name="a23_bank")
        first_product(a0_lo[:], 0, slice(0, half))
        first_product(a0_hi[:], 0, slice(half, J))
        nc.scalar.copy(out=a_rows[0][:, 0:half], in_=a0_lo[:])
        nc.vector.tensor_copy(out=a_rows[0][:, half:J], in_=a0_hi[:])
        first_product(a1_bank[:], 1, slice(0, J))
        nc.vector.tensor_copy(out=a_rows[1][:], in_=a1_bank[:])
        for t in (2, 3):
            first_product(a23_bank[:, t - 2, :], t, slice(0, J))
        for t in (2, 3):
            nc.vector.tensor_copy(out=a_rows[t][:], in_=a23_bank[:, t - 2, :])
        for t in range(PACK):
            nc.scalar.activation(out=boards[t][:].indirect(list3[:]), in_=a_rows[t][:], func=ACT.Copy)

        w2_codes = sb.tile([P, R], I32, name="w2_codes", align_bytes=64)
        w2_plane = sb.tile([P, R], U8, name="w2_plane", align_bytes=64)
        x2_plane = sb.tile([P, J], U8, name="x2_plane", align_bytes=64)
        x2_words = sb.tile([P, J], U32, name="x2_words", align_bytes=64)
        nc.vector.tensor_copy(out=x2_plane[:], in_=x_plane[:].indirect(list2[:]))
        nc.vector.tensor_copy(out=x2_words[:], in_=x_words[:].bitcast(U32).indirect(list2[:]))
        dst, src = deal_views(w2_plane[:], w2_plane_raw[:], LINE)
        nc.vector.tensor_copy(out=dst, in_=src)
        dst, src = deal_views(w2_codes[:], w2_raw[:], LINE // 4)
        nc.vector.tensor_copy(out=dst, in_=src)
        b_rows = [sb.tile([P, J], F32, name="b%d" % t, align_bytes=64) for t in range(PACK)]
        for pair in range(2):
            b_bank = ps.tile([P, 2, J], F32, name="b_bank%d" % pair)
            for u in range(2):
                t = 2 * pair + u
                nc.tensor.matmul_mx(
                    out=b_bank[:, u, :],
                    lhsT=w2_codes[:, P * t : P * (t + 1)].bitcast(E5M2),
                    lhsT_scale=w2_plane[:, P * t : P * (t + 1)],
                    rhs=x2_words[:].bitcast(E4M3),
                    rhs_scale=x2_plane[:],
                    start=True,
                    stop=True,
                )
            for u in range(2):
                nc.vector.tensor_copy(out=b_rows[2 * pair + u][:], in_=b_bank[:, u, :])

        hid = sb.tile([P, O, PACK], BF16, name="hid", align_bytes=64)
        hid_codes = sb.tile([P, O], U32, name="hid_codes", align_bytes=64)
        hid_plane = sb.tile([P, O], U8, name="hid_plane", align_bytes=64)
        picked = [sb.tile([P, 2, O], F32, name="picked%d" % pair, align_bytes=64) for pair in range(2)]
        gate = [sb.tile([P, 2, O], F32, name="gate%d" % pair, align_bytes=64) for pair in range(2)]

        def pick(t):
            nc.scalar.activation(
                out=picked[t // 2][:, t % 2, :], in_=boards[t][:].indirect(list4[:]), func=ACT.Copy,
                scale=sa_t[:, t : t + 1],
            )

        def look(t, lo, hi):
            nc.scalar.activation(
                out=gate[t // 2][:, t % 2, lo:hi], in_=b_rows[t][:].indirect(list5[:, lo // 16 : hi // 16]),
                func=ACT.Sigmoid, bias=bg_t[:, t : t + 1], scale=sg_t[:, t : t + 1],
            )

        def join(pair, lo, hi):
            nc.vector.tensor_tensor(
                out=hid[:, lo:hi, 2 * pair : 2 * pair + 2],
                in0=picked[pair][:, :, lo:hi].rearrange("p u o -> p o u"),
                in1=gate[pair][:, :, lo:hi].rearrange("p u o -> p o u"),
                op=ALU.mult,
            )

        halves = ((0, O // 2), (O // 2, O))
        for t in range(PACK - 1):
            pick(t)
            look(t, 0, O)
            if t == 1:
                join(0, 0, O)
        pick(PACK - 1)
        for lo, hi in halves:
            look(PACK - 1, lo, hi)
            join(1, lo, hi)
        for lo, hi in halves:
            nc.vector.quantize_mx(
                out=hid_codes[:, lo:hi].bitcast(E4M3),
                scales=hid_plane[:, lo:hi],
                in_=hid[:, lo:hi, :].rearrange("p o t -> p (o t)"),
            )
        for h in range(N // P):
            o_bank = ps.tile([P, O], F32, name="o_bank%d" % h)
            result = sb.tile([P, O], F32, name="result%d" % h, align_bytes=64)
            nc.tensor.matmul_mx(
                out=o_bank[:],
                lhsT=wb_codes[:, P * h : P * (h + 1)].bitcast(E5M2),
                lhsT_scale=wb_plane[:, P * h : P * (h + 1)],
                rhs=hid_codes[:].bitcast(E4M3),
                rhs_scale=hid_plane[:],
                start=True,
                stop=True,
            )
            if h == 0:
                nc.scalar.copy(out=result[:], in_=o_bank[:])
                nc.scalar.dma_start(out=out[P * h : P * (h + 1), :], in_=result[:])
            else:
                nc.vector.tensor_copy(out=result[:], in_=o_bank[:])
                nc.sync.dma_start(out=out[P * h : P * (h + 1), :], in_=result[:])
